import numpy as np, ml_dtypes
CORES = [14,30,46,142,158,174,270,286,302,398,414,430]
N = 12
TK = 128
def gelu(z): return 0.5 * z * (1.0 + np.tanh(0.7978845608028654 * (z + 0.044715 * z ** 3)))
def setup_inputs(rng):
    return {"x": rng.standard_normal((N, 128, TK), dtype=np.float32).astype(ml_dtypes.bfloat16), "w1": (rng.standard_normal((N, 128, 128), dtype=np.float32) / 8).astype(ml_dtypes.bfloat16), "w2": (rng.standard_normal((N, 128, 128), dtype=np.float32) / 8).astype(ml_dtypes.bfloat16)}
def setup_inputs_big(rng):
    d = setup_inputs(rng)
    for k in ("x",): d[k] = (d[k].astype(np.float32) * 1024.0).astype(d[k].dtype)
    return d
def setup_inputs_small(rng):
    d = setup_inputs(rng)
    for k in ("x",): d[k] = (d[k].astype(np.float32) * (1 / 1024.0)).astype(d[k].dtype)
    return d
def setup_inputs_apart(rng):
    d = setup_inputs(rng)
    f = (10.0 ** rng.permutation(np.linspace(-1.5, 1.5, N))).astype(np.float32).reshape(N, 1, 1)
    for k in ("x",): d[k] = (d[k].astype(np.float32) * f).astype(d[k].dtype)
    return d
def reference(x, w1, w2):
    X, W1, W2 = x.astype(np.float64), w1.astype(np.float64), w2.astype(np.float64)
    y = np.zeros((N, 128, TK))
    for r in range(N):
        for j in range(N):
            y[r] += W2[j].T @ (gelu(W1[j].T @ X[r]))
    return {"y": y.astype(ml_dtypes.bfloat16)}

@@ -1,0 +1,125 @@
+import comms_topo
+from concourse.bass import DstId, RemoteDMATransfer
+from concourse.mybir import AluOpType, ActivationFunctionType
+
+CORES = [14, 30, 46, 142, 158, 174, 270, 286, 302, 398, 414, 430]
+D = 128
+W = 2 * D
+_RACKS = [comms_topo.rack(comms_topo.host(c)) for c in CORES]
+G = max(_RACKS.count(k) for k in _RACKS)
+NB = 4
+BANK = 512
+
+SCRATCH = {
+    "wall": ("sbuf", [128, G * W], "bfloat16"),
+    "xown": ("sbuf", [128, D], "bfloat16"),
+    "xin": ("sbuf", [128, D], "bfloat16"),
+    "hsb": ("sbuf", [128, 2 * G * D], "bfloat16"),
+    "ypsb": ("sbuf", [128, D], "bfloat16"),
+    "yin": ("sbuf", [128, D], "bfloat16"),
+    "ysb": ("sbuf", [128, D], "bfloat16"),
+    "yp": ("psum", [128, BANK], "float32"),
+    "yo": ("psum", [128, BANK], "float32"),
+}
+for _b in range(NB):
+    SCRATCH["hp%d" % _b] = ("psum", [128, BANK], "float32")
+
+SEMAPHORES = (["xl", "wl", "xarr", "ydp", "ydo", "ypc", "yarr", "yadd", "st", "sent"]
+              + ["ws%d" % s for s in range(G)]
+              + ["m%d" % k for k in range(2 * G)]
+              + ["a%d" % k for k in range(2 * G)])
+
+
+def _engines(mask):
+    return bin(mask).count("1")
+
+
+def rank_program(g, core, T, topo):
+    if T.rank_of(core) is None:
+        return
+    sem = T.sem
+    te, sc, ve, sy = g.tensor, g.scalar, g.vector, g.sync
+
+    my_rack = topo.rack(topo.host(core))
+    ring = [c for c in T.cores if topo.rack(topo.host(c)) == my_rack]
+    n = len(ring)
+    i = ring.index(core)
+    partner = [c for c in T.cores if topo.rack(topo.host(c)) != my_rack
+               and topo.chip(c) == topo.chip(core) and topo.may_write(core, c)][0]
+
+    def slot(s):
+        return T.wall[:, s * W:(s + 1) * W]
+
+    sy.dma_start(T.xown[:], T.x[:]).then_inc(sem.xl, 16)
+    sc.dma_start(T.wall[:, i * W:i * W + D], T.w1[:]).then_inc(sem.wl, 16)
+    sy.dma_start(T.wall[:, i * W + D:(i + 1) * W], T.w2[:]).then_inc(sem.wl, 16)
+
+    prid, ppid = topo.addr(partner, core)
+    pmask = topo.mask(core, partner)
+    sent = 0
+    g.wait_ge(sem.xl, 16)
+    g.remote_dma(out_ap=T.xin[:], in_ap=T.xown[:], remote_sem=sem.xarr, local_sem=sem.sent,
+                 pid=ppid, routing_id=prid, dma_engine_mask=pmask)
+    sent += _engines(pmask)
+
+    dsts = [ring[(i + o) % n] for o in range(1, n)]
+    wmask = topo.mask(core, dsts[0])
+    for d in dsts:
+        wmask &= topo.mask(core, d)
+    ids = []
+    for d in dsts:
+        rid, pid = topo.addr(d, core)
+        ids.append(DstId(rid=rid, pnc=pid))
+    g.wait_ge(sem.wl, 32)
+    g.remote_dma_fused([RemoteDMATransfer(dst_ids=ids, dma_engine_mask=wmask, remote_sem=sem["ws%d" % i],
+                                          srcs=[slot(i)], dsts=[slot(i) for _ in dsts], alu_op=0)],
+                       local_sem=sem.sent)
+    sent += _engines(wmask)
+
+    xs = {"p": T.xin[:], "o": T.xown[:]}
+    acc = {"p": T.yp[:, 0:D], "o": T.yo[:, 0:D]}
+    done = {"p": sem.ydp, "o": sem.ydo}
+    k = 0
+    for step in range(n):
+        s = (i - step) % n
+        w1 = T.wall[:, s * W:s * W + D]
+        w2 = T.wall[:, s * W + D:(s + 1) * W]
+        if step == 0:
+            te.wait_ge(sem.wl, 32)
+            te.wait_ge(sem.xl, 16)
+            blocks = ["o", "p"]
+        else:
+            src = ring[s]
+            te.wait_ge(sem["ws%d" % s], _engines(topo.mask(src, core)))
+            blocks = ["p", "o"]
+        mine = []
+        for b in blocks:
+            if step == 0 and b == "p":
+                te.wait_ge(sem.xarr, _engines(topo.mask(partner, core)))
+            hp = T["hp%d" % (k % NB)][:, 0:D]
+            hs = T.hsb[:, k * D:(k + 1) * D]
+            te.matmul(hp, w1, xs[b], True, True).then_inc(sem["m%d" % k], 1)
+            sc.wait_ge(sem["m%d" % k], 1)
+            sc.activation(hs, hp, ActivationFunctionType.Gelu_apprx_tanh).then_inc(sem["a%d" % k], 1)
+            mine.append((b, k, hs))
+            k += 1
+        for b, kk, hs in mine:
+            te.wait_ge(sem["a%d" % kk], 1)
+            mm = te.matmul(acc[b], w2, hs, step == 0, step == n - 1)
+            if step == n - 1:
+                mm.then_inc(done[b], 1)
+
+    ve.wait_ge(sem.ydp, 1)
+    ve.tensor_copy(T.ypsb[:], T.yp[:, 0:D]).then_inc(sem.ypc, 1)
+    g.wait_ge(sem.ypc, 1)
+    g.remote_dma(out_ap=T.yin[:], in_ap=T.ypsb[:], remote_sem=sem.yarr, local_sem=sem.sent,
+                 pid=ppid, routing_id=prid, dma_engine_mask=pmask)
+    sent += _engines(pmask)
+
+    ve.wait_ge(sem.ydo, 1)
+    ve.wait_ge(sem.yarr, _engines(topo.mask(partner, core)))
+    ve.tensor_tensor(T.ysb[:], T.yo[:, 0:D], T.yin[:], AluOpType.add).then_inc(sem.yadd, 1)
+    sy.wait_ge(sem.yadd, 1)
+    sy.dma_start(T.y[:], T.ysb[:]).then_inc(sem.st, 16)
+    sy.wait_ge(sem.st, 16)
+    g.wait_ge(sem.sent, sent)

@@ -4,30 +4,33 @@ from concourse.mybir import AluOpType, ActivationFunctionType
 
 CORES = [14, 30, 46, 142, 158, 174, 270, 286, 302, 398, 414, 430]
 D = 128
+H = D // 2
 W = 2 * D
 _RACKS = [comms_topo.rack(comms_topo.host(c)) for c in CORES]
 G = max(_RACKS.count(k) for k in _RACKS)
-NB = 4
+NB = 3
+NH = 2 * G + 1
 BANK = 512
 
 SCRATCH = {
     "wall": ("sbuf", [128, G * W], "bfloat16"),
     "xown": ("sbuf", [128, D], "bfloat16"),
     "xin": ("sbuf", [128, D], "bfloat16"),
-    "hsb": ("sbuf", [128, 2 * G * D], "bfloat16"),
+    "hsb": ("sbuf", [128, NH * D], "bfloat16"),
     "ypsb": ("sbuf", [128, D], "bfloat16"),
     "yin": ("sbuf", [128, D], "bfloat16"),
     "ysb": ("sbuf", [128, D], "bfloat16"),
-    "yp": ("psum", [128, BANK], "float32"),
+    "yp0": ("psum", [128, BANK], "float32"),
+    "yp1": ("psum", [128, BANK], "float32"),
     "yo": ("psum", [128, BANK], "float32"),
 }
 for _b in range(NB):
     SCRATCH["hp%d" % _b] = ("psum", [128, BANK], "float32")
 
-SEMAPHORES = (["xl", "wl", "xarr", "ydp", "ydo", "ypc", "yarr", "yadd", "st", "sent"]
+SEMAPHORES = (["xl", "wl", "xarr", "yd0", "yd1", "ydo", "ypc0", "ypc1", "yarr", "yadd", "st", "sent"]
               + ["ws%d" % s for s in range(G)]
-              + ["m%d" % k for k in range(2 * G)]
-              + ["a%d" % k for k in range(2 * G)])
+              + ["m%d" % k for k in range(NH)]
+              + ["a%d" % k for k in range(NH)])
 
 
 def _engines(mask):
@@ -64,10 +67,9 @@ def rank_program(g, core, T, topo):
 
     dsts = [ring[(i + o) % n] for o in range(1, n)]
     wmask = topo.mask(core, dsts[0])
-    for d in dsts:
-        wmask &= topo.mask(core, d)
     ids = []
     for d in dsts:
+        wmask &= topo.mask(core, d)
         rid, pid = topo.addr(d, core)
         ids.append(DstId(rid=rid, pnc=pid))
     g.wait_ge(sem.wl, 32)
@@ -76,42 +78,66 @@ def rank_program(g, core, T, topo):
                        local_sem=sem.sent)
     sent += _engines(wmask)
 
-    xs = {"p": T.xin[:], "o": T.xown[:]}
-    acc = {"p": T.yp[:, 0:D], "o": T.yo[:, 0:D]}
-    done = {"p": sem.ydp, "o": sem.ydo}
-    k = 0
-    for step in range(n):
-        s = (i - step) % n
-        w1 = T.wall[:, s * W:s * W + D]
-        w2 = T.wall[:, s * W + D:(s + 1) * W]
-        if step == 0:
-            te.wait_ge(sem.wl, 32)
-            te.wait_ge(sem.xl, 16)
-            blocks = ["o", "p"]
-        else:
-            src = ring[s]
-            te.wait_ge(sem["ws%d" % s], _engines(topo.mask(src, core)))
-            blocks = ["p", "o"]
-        mine = []
-        for b in blocks:
-            if step == 0 and b == "p":
-                te.wait_ge(sem.xarr, _engines(topo.mask(partner, core)))
-            hp = T["hp%d" % (k % NB)][:, 0:D]
-            hs = T.hsb[:, k * D:(k + 1) * D]
-            te.matmul(hp, w1, xs[b], True, True).then_inc(sem["m%d" % k], 1)
-            sc.wait_ge(sem["m%d" % k], 1)
-            sc.activation(hs, hp, ActivationFunctionType.Gelu_apprx_tanh).then_inc(sem["a%d" % k], 1)
-            mine.append((b, k, hs))
-            k += 1
-        for b, kk, hs in mine:
-            te.wait_ge(sem["a%d" % kk], 1)
-            mm = te.matmul(acc[b], w2, hs, step == 0, step == n - 1)
-            if step == n - 1:
-                mm.then_inc(done[b], 1)
+    def arr(o):
+        s = (i - o) % n
+        return ("w", sem["ws%d" % s], _engines(topo.mask(ring[s], core)))
 
-    ve.wait_ge(sem.ydp, 1)
-    ve.tensor_copy(T.ypsb[:], T.yp[:, 0:D]).then_inc(sem.ypc, 1)
-    g.wait_ge(sem.ypc, 1)
+    last = n - 1
+    blk = {}
+    for o in range(n):
+        blk["o%d" % o] = ("o", o, 0, D)
+        blk["p%d" % o] = ("p", o, 0, D)
+    blk["pa"] = ("p", last, 0, H)
+    blk["pb"] = ("p", last, H, D)
+    seq = [("w", sem.wl, 32), ("w", sem.xl, 16), (1, "o0"),
+           ("w", sem.xarr, _engines(topo.mask(partner, core))), (1, "p0"), (2, "o0")]
+    for o in range(1, last):
+        seq += [arr(o), (1, "p%d" % o), (2, "p%d" % (o - 1))]
+    seq += [(1, "o1"), (2, "p%d" % (last - 1)),
+            arr(last), (1, "pa"), (1, "pb"), (2, "pa"), (2, "pb"),
+            (2, "o1"), (1, "o2")]
+    for o in range(3, n):
+        seq += [(1, "o%d" % o), (2, "o%d" % (o - 1))]
+    seq += [(2, "o%d" % last)]
+
+    xs = {"p": T.xin, "o": T.xown}
+    left = {"yp0": n, "yp1": n, "yo": n}
+    done = {"yp0": sem.yd0, "yp1": sem.yd1, "yo": sem.ydo}
+    num = {}
+    for op in seq:
+        if op[0] == "w":
+            te.wait_ge(op[1], op[2])
+            continue
+        b, o, c0, c1 = blk[op[1]]
+        s = (i - o) % n
+        if op[0] == 1:
+            k = len(num)
+            num[op[1]] = k
+            hp = T["hp%d" % (k % NB)][:, 0:c1 - c0]
+            te.matmul(hp, T.wall[:, s * W:s * W + D], xs[b][:, c0:c1], True, True).then_inc(sem["m%d" % k], 1)
+            sc.wait_ge(sem["m%d" % k], 1)
+            sc.activation(T.hsb[:, k * D:k * D + c1 - c0], hp,
+                          ActivationFunctionType.Gelu_apprx_tanh).then_inc(sem["a%d" % k], 1)
+            continue
+        k = num[op[1]]
+        te.wait_ge(sem["a%d" % k], 1)
+        if b == "o":
+            parts = [("yo", c0, c1)]
+        else:
+            parts = [(nm, lo, hi) for nm, lo, hi in (("yp0", 0, H), ("yp1", H, D)) if c0 <= lo and hi <= c1]
+        for nm, lo, hi in parts:
+            mm = te.matmul(T[nm][:, 0:hi - lo], T.wall[:, s * W + D:(s + 1) * W],
+                           T.hsb[:, k * D + lo - c0:k * D + hi - c0], left[nm] == n, left[nm] == 1)
+            left[nm] -= 1
+            if left[nm] == 0:
+                mm.then_inc(done[nm], 1)
+
+    ve.wait_ge(sem.yd0, 1)
+    ve.tensor_copy(T.ypsb[:, 0:H], T.yp0[:, 0:H]).then_inc(sem.ypc0, 1)
+    ve.wait_ge(sem.yd1, 1)
+    ve.tensor_copy(T.ypsb[:, H:D], T.yp1[:, 0:H]).then_inc(sem.ypc1, 1)
+    g.wait_ge(sem.ypc0, 1)
+    g.wait_ge(sem.ypc1, 1)
     g.remote_dma(out_ap=T.yin[:], in_ap=T.ypsb[:], remote_sem=sem.yarr, local_sem=sem.sent,
                  pid=ppid, routing_id=prid, dma_engine_mask=pmask)
     sent += _engines(pmask)

import comms_topo
from concourse.bass import DstId, RemoteDMATransfer
from concourse.mybir import AluOpType, ActivationFunctionType

CORES = [14, 30, 46, 142, 158, 174, 270, 286, 302, 398, 414, 430]
D = 128
H = D // 2
W = 2 * D
_RACKS = [comms_topo.rack(comms_topo.host(c)) for c in CORES]
G = max(_RACKS.count(k) for k in _RACKS)
NB = 3
NH = 2 * G + 1
BANK = 512

SCRATCH = {
    "wall": ("sbuf", [128, G * W], "bfloat16"),
    "xown": ("sbuf", [128, D], "bfloat16"),
    "xin": ("sbuf", [128, D], "bfloat16"),
    "hsb": ("sbuf", [128, NH * D], "bfloat16"),
    "ypsb": ("sbuf", [128, D], "bfloat16"),
    "yin": ("sbuf", [128, D], "bfloat16"),
    "ysb": ("sbuf", [128, D], "bfloat16"),
    "yp0": ("psum", [128, BANK], "float32"),
    "yp1": ("psum", [128, BANK], "float32"),
    "yo": ("psum", [128, BANK], "float32"),
}
for _b in range(NB):
    SCRATCH["hp%d" % _b] = ("psum", [128, BANK], "float32")

SEMAPHORES = (["xl", "wl", "xarr", "yd0", "yd1", "ydo", "ypc0", "ypc1", "yarr", "yadd", "st", "sent"]
              + ["ws%d" % s for s in range(G)]
              + ["m%d" % k for k in range(NH)]
              + ["a%d" % k for k in range(NH)])


def _engines(mask):
    return bin(mask).count("1")


def rank_program(g, core, T, topo):
    if T.rank_of(core) is None:
        return
    sem = T.sem
    te, sc, ve, sy = g.tensor, g.scalar, g.vector, g.sync

    my_rack = topo.rack(topo.host(core))
    ring = [c for c in T.cores if topo.rack(topo.host(c)) == my_rack]
    n = len(ring)
    i = ring.index(core)
    partner = [c for c in T.cores if topo.rack(topo.host(c)) != my_rack
               and topo.chip(c) == topo.chip(core) and topo.may_write(core, c)][0]

    def slot(s):
        return T.wall[:, s * W:(s + 1) * W]

    sy.dma_start(T.xown[:], T.x[:]).then_inc(sem.xl, 16)
    sc.dma_start(T.wall[:, i * W:i * W + D], T.w1[:]).then_inc(sem.wl, 16)
    sy.dma_start(T.wall[:, i * W + D:(i + 1) * W], T.w2[:]).then_inc(sem.wl, 16)

    prid, ppid = topo.addr(partner, core)
    pmask = topo.mask(core, partner)
    sent = 0
    g.wait_ge(sem.xl, 16)
    g.remote_dma(out_ap=T.xin[:], in_ap=T.xown[:], remote_sem=sem.xarr, local_sem=sem.sent,
                 pid=ppid, routing_id=prid, dma_engine_mask=pmask)
    sent += _engines(pmask)

    dsts = [ring[(i + o) % n] for o in range(1, n)]
    wmask = topo.mask(core, dsts[0])
    ids = []
    for d in dsts:
        wmask &= topo.mask(core, d)
        rid, pid = topo.addr(d, core)
        ids.append(DstId(rid=rid, pnc=pid))
    g.wait_ge(sem.wl, 32)
    g.remote_dma_fused([RemoteDMATransfer(dst_ids=ids, dma_engine_mask=wmask, remote_sem=sem["ws%d" % i],
                                          srcs=[slot(i)], dsts=[slot(i) for _ in dsts], alu_op=0)],
                       local_sem=sem.sent)
    sent += _engines(wmask)

    def arr(o):
        s = (i - o) % n
        return ("w", sem["ws%d" % s], _engines(topo.mask(ring[s], core)))

    last = n - 1
    blk = {}
    for o in range(n):
        blk["o%d" % o] = ("o", o, 0, D)
        blk["p%d" % o] = ("p", o, 0, D)
    blk["pa"] = ("p", last, 0, H)
    blk["pb"] = ("p", last, H, D)
    seq = [("w", sem.wl, 32), ("w", sem.xl, 16), (1, "o0"),
           ("w", sem.xarr, _engines(topo.mask(partner, core))), (1, "p0"), (2, "o0")]
    for o in range(1, last):
        seq += [arr(o), (1, "p%d" % o), (2, "p%d" % (o - 1))]
    seq += [(1, "o1"), (2, "p%d" % (last - 1)),
            arr(last), (1, "pa"), (1, "pb"), (2, "pa"), (2, "pb"),
            (2, "o1"), (1, "o2")]
    for o in range(3, n):
        seq += [(1, "o%d" % o), (2, "o%d" % (o - 1))]
    seq += [(2, "o%d" % last)]

    xs = {"p": T.xin, "o": T.xown}
    left = {"yp0": n, "yp1": n, "yo": n}
    done = {"yp0": sem.yd0, "yp1": sem.yd1, "yo": sem.ydo}
    num = {}
    for op in seq:
        if op[0] == "w":
            te.wait_ge(op[1], op[2])
            continue
        b, o, c0, c1 = blk[op[1]]
        s = (i - o) % n
        if op[0] == 1:
            k = len(num)
            num[op[1]] = k
            hp = T["hp%d" % (k % NB)][:, 0:c1 - c0]
            te.matmul(hp, T.wall[:, s * W:s * W + D], xs[b][:, c0:c1], True, True).then_inc(sem["m%d" % k], 1)
            sc.wait_ge(sem["m%d" % k], 1)
            sc.activation(T.hsb[:, k * D:k * D + c1 - c0], hp,
                          ActivationFunctionType.Gelu_apprx_tanh).then_inc(sem["a%d" % k], 1)
            continue
        k = num[op[1]]
        te.wait_ge(sem["a%d" % k], 1)
        if b == "o":
            parts = [("yo", c0, c1)]
        else:
            parts = [(nm, lo, hi) for nm, lo, hi in (("yp0", 0, H), ("yp1", H, D)) if c0 <= lo and hi <= c1]
        for nm, lo, hi in parts:
            mm = te.matmul(T[nm][:, 0:hi - lo], T.wall[:, s * W + D:(s + 1) * W],
                           T.hsb[:, k * D + lo - c0:k * D + hi - c0], left[nm] == n, left[nm] == 1)
            left[nm] -= 1
            if left[nm] == 0:
                mm.then_inc(done[nm], 1)

    ve.wait_ge(sem.yd0, 1)
    ve.tensor_copy(T.ypsb[:, 0:H], T.yp0[:, 0:H]).then_inc(sem.ypc0, 1)
    ve.wait_ge(sem.yd1, 1)
    ve.tensor_copy(T.ypsb[:, H:D], T.yp1[:, 0:H]).then_inc(sem.ypc1, 1)
    g.wait_ge(sem.ypc0, 1)
    g.wait_ge(sem.ypc1, 1)
    g.remote_dma(out_ap=T.yin[:], in_ap=T.ypsb[:], remote_sem=sem.yarr, local_sem=sem.sent,
                 pid=ppid, routing_id=prid, dma_engine_mask=pmask)
    sent += _engines(pmask)

    ve.wait_ge(sem.ydo, 1)
    ve.wait_ge(sem.yarr, _engines(topo.mask(partner, core)))
    ve.tensor_tensor(T.ysb[:], T.yo[:, 0:D], T.yin[:], AluOpType.add).then_inc(sem.yadd, 1)
    sy.wait_ge(sem.yadd, 1)
    sy.dma_start(T.y[:], T.ysb[:]).then_inc(sem.st, 16)
    sy.wait_ge(sem.st, 16)
    g.wait_ge(sem.sent, sent)
